import numpy as np
import ml_dtypes


def mxq(x, axis, fmt="e4m3"):
    dtype, down = {"e4m3": (ml_dtypes.float8_e4m3fn, 7), "e5m2": (ml_dtypes.float8_e5m2, 14)}[fmt]
    v = np.moveaxis(np.asarray(x, np.float32).astype(ml_dtypes.bfloat16).astype(np.float64), axis, -1)
    blocks = v.reshape(v.shape[:-1] + (-1, 32))
    amax = np.abs(blocks).max(-1, keepdims=True)
    byte = np.maximum(np.where(amax > 0, np.frexp(amax)[1] - 1 + 127, 0) - down, 1)
    scale = np.exp2(byte - 127.0)
    codes = (blocks / scale).astype(np.float32).astype(dtype).astype(np.float64)
    return np.moveaxis((codes * scale).reshape(v.shape), -1, axis)


WIDE = False


def mx_kscale(k):
    if not WIDE:
        return np.ones(k)
    levels = np.array([10, -10, 5, -5, 0])
    if k % 512:
        return np.exp2(np.random.permutation(np.resize(levels, k // 32))).repeat(32)
    a = np.empty((k // 512, 16))
    for p in range(k // 512):
        a[p, :8] = np.random.permutation(np.resize(levels, 8))
        for g in range(8):
            far = levels[np.abs(levels - a[p, g]) >= 10]
            a[p, g + 8] = far[np.random.randint(len(far))]
    return np.exp2(a.ravel()).repeat(32)


def f64(x):
    return np.asarray(x).astype(np.float64)


def striped(idx):
    return np.tile(idx.reshape(-1, 16).T, (8, 1)).astype(np.uint16)


def unstriped(offs):
    return offs[:16].T.reshape(-1).astype(np.int64)


E2M1 = np.array([0.0, 0.5, 1.0, 1.5, 2.0, 3.0, 4.0, 6.0, -0.0, -0.5, -1.0, -1.5, -2.0, -3.0, -4.0, -6.0])


def pack_weight(w, fmt):
    k, n = w.shape
    w = f64(np.asarray(w, np.float32).astype(ml_dtypes.bfloat16)).reshape(k // 32, 32, n)
    amax = np.abs(w).max(1)
    if fmt == "e4m3":
        byte = np.frexp(amax)[1] - 1 + 127 - 7
    else:
        mant, ex = np.frexp(amax / 6.0)
        byte = np.where(mant > 0.5, ex, ex - 1) + 127
    byte = np.clip(np.where(amax > 0, byte, 1), 1, 254)
    scaled = (w * np.exp2(127.0 - byte)[:, None, :]).reshape(k, n).astype(np.float32)
    by_word = np.ascontiguousarray(scaled.reshape(k // 512, 128, 4, n).transpose(0, 1, 3, 2))
    if fmt == "e4m3":
        words = by_word.astype(ml_dtypes.float8_e4m3fn).view(np.uint8)
    else:
        c = by_word.astype(ml_dtypes.float4_e2m1fn).view(np.uint8) & 0xF
        words = (c[..., 0::2] | (c[..., 1::2] << 4)).reshape(k // 512, 128, 2 * n)
    return np.ascontiguousarray(words), np.ascontiguousarray(byte.astype(np.uint8).reshape(k // 512, 16, n))


def unpack_weight(words, scales, fmt):
    g, _, n = scales.shape
    words = np.ascontiguousarray(words).reshape(g, 128, n, -1)
    if fmt == "e4m3":
        vals = words.view(ml_dtypes.float8_e4m3fn).astype(np.float64)
    else:
        nib = np.empty((g, 128, n, 4), np.uint8)
        nib[..., 0::2] = words & 0xF
        nib[..., 1::2] = words >> 4
        vals = E2M1[nib]
    vals = vals * np.repeat(np.exp2(scales.astype(np.float64) - 127.0), 8, axis=1)[..., None]
    return vals.transpose(0, 1, 3, 2).reshape(g * 512, n)


def planes(y):
    n, m = y.shape
    v = y.astype(np.float32).astype(ml_dtypes.bfloat16).astype(np.float64).reshape(n // 32, 32, m)
    top = np.abs(v).max(1)
    byte = np.clip(np.where(top > 0, np.frexp(top)[1] - 1 + 127 - 7, 1), 1, 254)
    codes = (v * np.exp2(127.0 - byte)[:, None, :]).reshape(n, m).astype(np.float32).astype(ml_dtypes.float8_e4m3fn).view(np.uint8)
    words = codes.reshape(n // 512, 128, 4, m).transpose(0, 1, 3, 2)
    return np.ascontiguousarray(words), np.ascontiguousarray(byte.astype(np.uint8).reshape(n // 512, 16, m))


def gelu(v):
    return 0.5 * v * (1.0 + np.tanh(np.sqrt(2.0 / np.pi) * (v + 0.044715 * v**3)))


K, T, E, C, H, HS, N = 512, 768, 3, 256, 512, 512, 512


def by_expert(wq, xq):
    return np.concatenate([wq[e].T @ xq[:, e * C:(e + 1) * C] for e in range(E)], axis=1)


def setup_inputs():
    n = np.random.standard_normal
    s = mx_kscale(K)
    u = mx_kscale(H)
    v = mx_kscale(HS)
    slot_token = np.random.permutation(T)[:E * C]
    x = pack_weight(n((K, T)) * s[:, None], "e4m3")
    w1 = [pack_weight(m, "e2m1") for m in n((E, K, H)) / np.sqrt(K) / s[None, :, None]]
    w3 = [pack_weight(m, "e2m1") for m in n((E, K, H)) / np.sqrt(K) / s[None, :, None] * u]
    w2 = [pack_weight(m, "e2m1") for m in n((E, H, N)) / np.sqrt(H) / u[None, :, None]]
    w1s = pack_weight(n((K, HS)) / np.sqrt(K) / s[:, None], "e4m3")
    w3s = pack_weight(n((K, HS)) / np.sqrt(K) / s[:, None] * v, "e4m3")
    w2s = pack_weight(n((HS, N)) / np.sqrt(HS) / v[:, None], "e4m3")
    return {
        "x_words": x[0],
        "x_scales": x[1],
        "w1_words": np.stack([m[0] for m in w1]),
        "w1_scales": np.stack([m[1] for m in w1]),
        "w3_words": np.stack([m[0] for m in w3]),
        "w3_scales": np.stack([m[1] for m in w3]),
        "w2_words": np.stack([m[0] for m in w2]),
        "w2_scales": np.stack([m[1] for m in w2]),
        "w1s_words": w1s[0],
        "w1s_scales": w1s[1],
        "w3s_words": w3s[0],
        "w3s_scales": w3s[1],
        "w2s_words": w2s[0],
        "w2s_scales": w2s[1],
        "gate": np.tile(np.random.uniform(0.2, 1.0, E * C), (128, 1)).astype(np.float32),
        "offs": striped(slot_token),
    }


def reference(x_words, x_scales, w1_words, w1_scales, w3_words, w3_scales, w2_words, w2_scales, w1s_words, w1s_scales, w3s_words, w3s_scales, w2s_words, w2s_scales, gate, offs):
    w1 = np.stack([unpack_weight(w1_words[e], w1_scales[e], "e2m1") for e in range(E)])
    w3 = np.stack([unpack_weight(w3_words[e], w3_scales[e], "e2m1") for e in range(E)])
    w2 = np.stack([unpack_weight(w2_words[e], w2_scales[e], "e2m1") for e in range(E)])
    w1s = unpack_weight(w1s_words, w1s_scales, "e4m3")
    w3s = unpack_weight(w3s_words, w3s_scales, "e4m3")
    w2s = unpack_weight(w2s_words, w2s_scales, "e4m3")
    idx = unstriped(offs)
    x = unpack_weight(x_words, x_scales, "e4m3")
    hs = gelu(w1s.T @ x) * (w3s.T @ x)
    ys = w2s.T @ mxq(hs, 0, "e4m3")
    h = gelu(by_expert(w1, x[:, idx])) * by_expert(w3, x[:, idx])
    y = by_expert(w2, mxq(h, 0, "e4m3"))
    c = np.zeros((N, T))
    c[:, idx] = f64(gate[:1]) * y
    out_0 = ys + c
    return (out_0,) + planes(out_0)

@@ -1,0 +1,390 @@
+from contextlib import ExitStack
+
+import concourse.mybir as mybir
+from concourse.masks import make_identity
+
+K, T, E, C, H, N = 512, 768, 3, 256, 512, 512
+FLOPS = 2 * (T + E * C) * (2 * K * H + H * N)
+
+F32 = mybir.dt.float32
+BF16 = mybir.dt.bfloat16
+I32 = mybir.dt.int32
+U32 = mybir.dt.uint32
+U16 = mybir.dt.uint16
+U8 = mybir.dt.uint8
+FP8X4 = mybir.dt.float8_e4m3fn_x4
+FP4X4 = mybir.dt.float4_e2m1fn_x4
+GELU = mybir.ActivationFunctionType.Gelu_apprx_tanh
+COPY = mybir.ActivationFunctionType.Copy
+MULT = mybir.AluOpType.mult
+ADD = mybir.AluOpType.add
+
+P = 128
+PACK = 4
+LIST_COLS = C // 16
+
+
+def tile_moe_shf_glu_gelu_kernel(
+    tc, x_words, x_scales, w1_words, w1_scales, w3_words, w3_scales, w2_words, w2_scales,
+    w1s_words, w1s_scales, w3s_words, w3s_scales, w2s_words, w2s_scales, gate, offs,
+    out_0, out_1, out_2,
+):
+    nc = tc.nc
+    with ExitStack() as ctx:
+        keep = ctx.enter_context(tc.tile_pool(name="keep", bufs=1))
+        work = ctx.enter_context(tc.tile_pool(name="work", bufs=2))
+        psum = ctx.enter_context(tc.psum_pool(name="psum", bufs=2))
+
+        def kept(name, shape, dtype):
+            return keep.tile(shape, dtype, name=name, align_bytes=64)
+
+        def load_words(name, src, width):
+            tile = kept(name, [P, width], U8)
+            nc.sync.dma_start(out=tile[:].bitcast(I32), in_=src.bitcast(I32))
+            return tile
+
+        def load_scale_rows(plane, first, src, groups):
+            for r in range(4):
+                nc.sync.dma_start(
+                    out=plane[first + r : P : 32, :].bitcast(I32).rearrange("q (g c) -> q g c", g=groups),
+                    in_=src[:, r:16:4, :].bitcast(I32).rearrange("g q c -> q g c"),
+                )
+
+        offsets = keep.tile([P, T // 16], U16, name="offsets")
+        x_plane = kept("x_plane", [P, T], U8)
+        w13_plane = kept("w13_plane", [P, 2 * E * H], U8)
+        w2_plane_raw = kept("w2_plane_raw", [P, (E - 1) * N], U8)
+        packed_raw = kept("packed_raw", [P, N], U8)
+        ident = kept("ident", [P, P], F32)
+        for plane in (x_plane, w13_plane, w2_plane_raw, packed_raw):
+            nc.vector.memset(plane[:].bitcast(I32), 0)
+
+        make_identity(nc, ident[:])
+
+        def stage_rows(queue, tile, sources, groups):
+            for i, src in enumerate(sources):
+                queue.dma_start(
+                    out=tile[:, i * groups * H : (i + 1) * groups * H].bitcast(I32).rearrange("b (g c) -> b g c", g=groups),
+                    in_=src.rearrange("g b c -> b g c").bitcast(I32),
+                )
+
+        def spread_rows(plane, tile):
+            for r in range(4):
+                nc.sync.dma_start(out=plane[r:P:32, :].bitcast(I32), in_=tile[r:16:4, :].bitcast(I32))
+
+        def load_experts(name, src, first):
+            count = E - first
+            tile = kept(name, [P, count, 2 * H], U8)
+            nc.sync.dma_start(
+                out=tile[:].bitcast(I32), in_=src[first:E].rearrange("e s p c -> p (e s) c").bitcast(I32)
+            )
+            return tile
+
+        by_group = "e s b c -> (e s) b c"
+        staged = kept("staged", [16, 2 * E * H], U8)
+        staged_packed = kept("staged_packed", [64, N], U8)
+
+        def stage_packed(queue):
+            for j, src in enumerate((w2_scales[E - 1, 0], w1s_scales[0], w3s_scales[0], w2s_scales[0])):
+                queue.dma_start(
+                    out=staged_packed[16 * j : 16 * j + 16, :].bitcast(I32),
+                    in_=src.rearrange("(q r) c -> r q c", r=4).bitcast(I32),
+                )
+
+        def spread_packed():
+            for q in range(4):
+                nc.sync.dma_start(
+                    out=packed_raw[32 * q : 32 * q + 16, :].bitcast(I32), in_=staged_packed[q:64:4, :].bitcast(I32)
+                )
+
+        x_tile = kept("x_tile", [P, T], I32)
+        gate_tile = kept("gate_tile", [P, T], F32)
+        stage_packed(nc.gpsimd)
+        nc.sync.dma_start(offsets[:], offs)
+        nc.sync.dma_start(out=x_tile[:], in_=x_words[0].rearrange("p t d -> p (t d)").bitcast(I32))
+        stage_rows(nc.sync, staged, (w1_scales.rearrange(by_group), w3_scales.rearrange(by_group)), E)
+        load_scale_rows(x_plane, 0, x_scales, 1)
+        w1_first = load_words("w1_first", w1_words[0, 0], 2 * H)
+        w3_first = load_words("w3_first", w3_words[0, 0], 2 * H)
+        spread_rows(w13_plane, staged)
+        w1_rest = load_experts("w1_rest", w1_words, 1)
+        w3_rest = load_experts("w3_rest", w3_words, 1)
+        w2_raw = load_experts("w2_raw", w2_words, 0)
+        load_scale_rows(w2_plane_raw, 0, w2_scales[0 : E - 1].rearrange(by_group), E - 1)
+        spread_packed()
+        w1s_tile = load_words("w1s_tile", w1s_words[0].rearrange("p c d -> p (c d)"), PACK * H)
+        nc.sync.dma_start(out=gate_tile[:], in_=gate)
+        w3s_tile = load_words("w3s_tile", w3s_words[0].rearrange("p c d -> p (c d)"), PACK * H)
+        w2s_raw = load_words("w2s_raw", w2s_words[0].rearrange("p c d -> p (c d)"), PACK * N)
+
+        w1_of = [w1_first[:], w1_rest[:, 0, :], w1_rest[:, 1, :]]
+        w3_of = [w3_first[:], w3_rest[:, 0, :], w3_rest[:, 1, :]]
+
+        windows = {}
+        holds = {}
+        counter = [0]
+
+        def act_tile(shape):
+            n = counter[0]
+            counter[0] = n + 1
+            return keep.tile(shape, F32, name="act%d" % n, tag=holds.get(n, "act%d" % n), align_bytes=64)
+
+        def window(t):
+            if t not in windows:
+                windows[t] = keep.tile([P, T], F32, name="window%d" % t, tag="window%d" % t, align_bytes=64)
+            return windows[t]
+
+        def gather(e):
+            lists = offsets[:, e * LIST_COLS : (e + 1) * LIST_COLS]
+            words = kept("slot_words%d" % e, [P, C], U32)
+            scales = kept("slot_scales%d" % e, [P, C], U8)
+            nc.vector.tensor_copy(words[:], x_tile[:].bitcast(U32).indirect(lists))
+            nc.vector.tensor_copy(scales[:], x_plane[:].indirect(lists))
+            return words[:], scales[:]
+
+        def deal(copy, out, in_):
+            copy(out=out.rearrange("p (t m) -> p t m", t=PACK), in_=in_.rearrange("p (m t) -> p t m", t=PACK))
+
+        w2_dealt = [kept("w2_words%d" % e, [P, 2 * N], U8) for e in range(E)]
+        w2_plane = [kept("w2_plane%d" % e, [P, N], U8) for e in range(E)]
+        w2s = kept("w2s", [P, N], U32)
+        w1s = kept("w1s", [P, H], U32)
+        w3s = kept("w3s", [P, H], U32)
+        packed = w2_plane[E - 1]
+
+        def deal_words(e, copy):
+            deal(copy, w2_dealt[e][:].bitcast(U16), w2_raw[:, e, :].bitcast(U16))
+
+        def deal_scales(e, copy):
+            deal(copy, w2_plane[e][:], w2_plane_raw[:, e * N : (e + 1) * N] if e < E - 1 else packed_raw[:])
+
+        h_codes = [kept("h_codes%d" % e, [P, C], U32) for e in range(E)]
+        h_plane = [kept("h_plane%d" % e, [P, C], U8) for e in range(E)]
+        hs_codes = kept("hs_codes", [P, T], U32)
+        hs_plane = kept("hs_plane", [P, T], U8)
+        slots = {}
+        turned = {}
+
+        def operands(chunk):
+            i = chunk[1]
+            return (slots[i][0], slots[i][1], w1_of[i].bitcast(FP4X4), w13_plane[:, i * H : (i + 1) * H],
+                    w3_of[i].bitcast(FP4X4), w13_plane[:, (E + i) * H : (E + i + 1) * H], h_codes[i][:], h_plane[i][:])
+
+        def first_layer(chunk, j):
+            tokens, token_scales, w1, w1_plane, w3, w3_plane = operands(chunk)[:6]
+            if j == 0:
+                turned[chunk] = psum.tile([P, 2, 2, P], F32, name="turned", tag="turned", bufs=1)
+            cols = slice(j * P, (j + 1) * P)
+            a1 = psum.tile([P, H], F32, name="a1", tag="a1", bufs=3)
+            a3 = psum.tile([P, H], F32, name="a3", tag="a3", bufs=2)
+            for acc, w, w_plane in ((a1, w1, w1_plane), (a3, w3, w3_plane)):
+                nc.tensor.matmul_mx(
+                    out=acc[:], lhsT=tokens[:, cols].bitcast(FP8X4), lhsT_scale=token_scales[:, cols],
+                    rhs=w, rhs_scale=w_plane, start=True, stop=True,
+                )
+            act = act_tile([P, 2, P, 2])
+            nc.scalar.activation(act[:], a1[:].rearrange("s (p u e) -> s u p e", u=2, e=2), GELU)
+            h = work.tile([P, 2, P, 2], BF16, name="h", tag="h")
+            nc.vector.tensor_tensor(h[:], a3[:].rearrange("s (p u e) -> s u p e", u=2, e=2), act[:], MULT)
+            for u in range(2):
+                nc.tensor.transpose(
+                    turned[chunk][:, j, u, :], h[:, u].rearrange("s p e -> s (p e)").bitcast(F32), ident[:]
+                )
+
+        def quantise_hidden(chunk, copy):
+            codes, plane = operands(chunk)[6:]
+            grouped = work.tile([P, C * PACK], BF16, name="grouped", tag="grouped", align_bytes=64)
+            copy(
+                out=grouped[:].bitcast(F32).rearrange("p (j s u) -> p j s u", j=2, u=2),
+                in_=turned[chunk][:].rearrange("p j u s -> p j s u"),
+            )
+            nc.vector.quantize_mx(out=codes.bitcast(FP8X4), scales=plane, in_=grouped[:])
+
+        shared_grouped = {}
+
+        shared_act = {}
+
+        def shared_sums(acc, w, first, c, j):
+            cols = slice(c * C + j * P, c * C + (j + 1) * P)
+            for t in range(PACK):
+                nc.tensor.matmul_mx(
+                    out=acc[:, t, :], lhsT=w[:, t * P : (t + 1) * P].bitcast(FP8X4),
+                    lhsT_scale=packed[first:P, t * P : (t + 1) * P],
+                    rhs=x_tile[:, cols].bitcast(FP8X4), rhs_scale=x_plane[:, cols], start=True, stop=True,
+                )
+
+        def shared_gelu(c, j):
+            a1 = psum.tile([P, PACK, P], F32, name="a1", tag="a1", bufs=3)
+            shared_sums(a1, w1s, 4, c, j)
+            shared_act[c, j] = act_tile([P, P, PACK])
+            nc.scalar.activation(shared_act[c, j][:], a1[:].rearrange("p t n -> p n t"), GELU)
+
+        def shared_hidden(c, j):
+            a3 = psum.tile([P, PACK, P], F32, name="a3", tag="a3", bufs=2)
+            shared_sums(a3, w3s, 8, c, j)
+            if j == 0:
+                shared_grouped[c] = work.tile([P, 2, P, PACK], BF16, name="grouped", tag="grouped", align_bytes=64)
+            nc.vector.tensor_tensor(shared_grouped[c][:, j], a3[:].rearrange("p t n -> p n t"), shared_act[c, j][:], MULT)
+
+        def quantise_shared(c):
+            cols = slice(c * C, (c + 1) * C)
+            nc.vector.quantize_mx(
+                out=hs_codes[:, cols].bitcast(FP8X4), scales=hs_plane[:, cols],
+                in_=shared_grouped[c][:].rearrange("p j n t -> p (j n t)"),
+            )
+
+        gated = {}
+        sums = {}
+
+        def second_layer(e, pair):
+            y = psum.tile([P, 2, C], F32, name="y", tag="y", bufs=2)
+            for i in range(2):
+                t = 2 * pair + i
+                nc.tensor.matmul_mx(
+                    out=y[:, i, :], lhsT=w2_dealt[e][:, t * 2 * P : (t + 1) * 2 * P].bitcast(FP4X4),
+                    lhsT_scale=w2_plane[e][:, t * P : (t + 1) * P],
+                    rhs=h_codes[e][:].bitcast(FP8X4), rhs_scale=h_plane[e][:], start=True, stop=True,
+                )
+            sums[e, pair] = y
+
+        def weigh(e, t):
+            gated[e, t] = kept("gated%d_%d" % (e, t), [P, C], F32)
+            nc.vector.tensor_tensor(gated[e, t][:], sums[e, t // 2][:, t % 2, :], gate_tile[:, e * C : (e + 1) * C], MULT)
+
+        def weigh_pair(e, pair):
+            both = keep.tile([P, 2, C], F32, name="gated%d_pair%d" % (e, pair), tag="gated%d%d" % (e, pair), align_bytes=64)
+            gates = gate_tile[:, e * C : (e + 1) * C].unsqueeze(1).to_broadcast([P, 2, C])
+            nc.vector.tensor_tensor(both[:], sums[e, pair][:], gates, MULT)
+            for i in range(2):
+                gated[e, 2 * pair + i] = both[:, i, :]
+
+        def plain(e, t):
+            gated[e, t] = kept("plain%d_%d" % (e, t), [P, C], F32)
+            nc.scalar.copy(out=gated[e, t][:], in_=sums[e, t // 2][:, t % 2, :])
+
+        def scatter_weighed(e, t):
+            lists = offsets[:, e * LIST_COLS : (e + 1) * LIST_COLS]
+            nc.vector.tensor_tensor(window(t)[:].indirect(lists), gated[e, t][:], gate_tile[:, e * C : (e + 1) * C], MULT)
+
+        def scatter(e, t, engine):
+            lists = offsets[:, e * LIST_COLS : (e + 1) * LIST_COLS]
+            values = gated[e, t][:]
+            if engine == "V":
+                nc.vector.tensor_copy(window(t)[:].indirect(lists), values)
+            else:
+                nc.scalar.activation(window(t)[:].indirect(lists), values, COPY)
+
+        V, S, G = nc.vector.tensor_copy, nc.scalar.copy, nc.gpsimd.tensor_copy
+        slots[0] = gather(0)
+        slots[1] = gather(1)
+        slots[2] = gather(2)
+        first_layer(("e", 0), 0)
+        deal_words(0, V)
+        first_layer(("e", 0), 1)
+        deal_scales(0, V)
+        quantise_hidden(("e", 0), S)
+        second_layer(0, 1)
+        second_layer(0, 0)
+        first_layer(("e", 1), 0)
+        first_layer(("e", 1), 1)
+        deal_scales(2, V)
+        deal(V, w1s[:], w1s_tile[:].bitcast(U32))
+        weigh_pair(0, 1)
+        quantise_hidden(("e", 1), S)
+        first_layer(("e", 2), 0)
+        first_layer(("e", 2), 1)
+        shared_gelu(0, 0)
+        shared_gelu(0, 1)
+        shared_gelu(1, 0)
+        shared_gelu(1, 1)
+        shared_gelu(2, 0)
+        shared_gelu(2, 1)
+        quantise_hidden(("e", 2), S)
+        weigh_pair(0, 0)
+        deal_words(1, V)
+        deal_scales(1, V)
+        second_layer(1, 1)
+        second_layer(1, 0)
+        deal(V, w3s[:], w3s_tile[:].bitcast(U32))
+        shared_hidden(0, 0)
+        shared_hidden(0, 1)
+        weigh_pair(1, 1)
+        quantise_shared(0)
+        shared_hidden(1, 0)
+        shared_hidden(1, 1)
+        weigh_pair(1, 0)
+        deal_words(2, V)
+        second_layer(2, 1)
+        second_layer(2, 0)
+        quantise_shared(1)
+        deal(V, w2s[:], w2s_raw[:].bitcast(U32))
+        shared_hidden(2, 0)
+        shared_hidden(2, 1)
+        scatter(0, 0, "V")
+        weigh_pair(2, 1)
+        scatter(1, 0, "V")
+        weigh_pair(2, 0)
+        quantise_shared(2)
+        scatter(2, 0, "V")
+        scatter(0, 3, "S")
+        scatter(0, 2, "S")
+        scatter(0, 1, "S")
+        scatter(1, 3, "S")
+        scatter(1, 2, "S")
+        scatter(1, 1, "S")
+        scatter(2, 3, "S")
+        scatter(2, 2, "S")
+        scatter(2, 1, "S")
+
+        def shared_product(out, t, cols):
+            nc.tensor.matmul_mx(
+                out=out, lhsT=w2s[:, t * P : (t + 1) * P].bitcast(FP8X4),
+                lhsT_scale=packed[12:P, t * P : (t + 1) * P],
+                rhs=hs_codes[:, cols].bitcast(FP8X4), rhs_scale=hs_plane[:, cols], start=True, stop=True,
+            )
+
+        narrow = [psum.tile([P, 2, C], F32, name="ys_narrow%d" % i, tag="y", bufs=2) for i in range(2)]
+        wide = [psum.tile([P, 2 * C], F32, name="ys_wide%d" % t, tag=("a1", "a3")[t % 2], bufs=(3, 2)[t % 2]) for t in range(PACK)]
+        result = kept("result", [P, PACK, T], F32)
+        out_rows = out_0.rearrange("(p t) n -> p t n", t=PACK)
+        order = (0, 3, 2, 1)
+        for t in order:
+            shared_product(wide[t][:], t, slice(0, 2 * C))
+            shared_product(narrow[t // 2][:, t % 2, :], t, slice(2 * C, T))
+        out_codes = kept("out_codes", [P, T], U32)
+        out_plane = kept("out_plane", [P, T], U8)
+        out_words = out_1[0].rearrange("p t d -> p (t d)").bitcast(I32)
+
+        def add(t, c):
+            cols = slice(c * C, (c + 1) * C)
+            ys = narrow[t // 2][:, t % 2, :] if c == 2 else wide[t][:, cols]
+            nc.vector.tensor_tensor(result[:, t, cols], ys, windows[t][:, cols], ADD)
+
+        for t in order[:3]:
+            nc.vector.tensor_tensor(result[:, t, 0 : 2 * C], wide[t][:], windows[t][:, 0 : 2 * C], ADD)
+            add(t, 2)
+            nc.sync.dma_start(out=out_rows[:, t, :], in_=result[:, t, :])
+        rounded = [kept("rounded%d" % c, [P, C, PACK], BF16) for c in range(E)]
+
+        def finish(c):
+            cols = slice(c * C, (c + 1) * C)
+            nc.vector.quantize_mx(
+                out=out_codes[:, cols].bitcast(FP8X4), scales=out_plane[:, cols],
+                in_=rounded[c][:].rearrange("p n t -> p (n t)"),
+            )
+            nc.sync.dma_start(out=out_words[:, cols], in_=out_codes[:, cols].bitcast(I32))
+
+        for c in range(E):
+            add(order[3], c)
+            if c < 1:
+                S(out=rounded[c][:], in_=result[:, :, c * C : (c + 1) * C].rearrange("p t n -> p n t"))
+        nc.sync.dma_start(out=out_rows[:, order[3], :], in_=result[:, order[3], :])
+        for c in (1, 2):
+            V(out=rounded[c][:], in_=result[:, :, c * C : (c + 1) * C].rearrange("p t n -> p n t"))
+        for c in range(E):
+            finish(c)
+        for q in range(4):
+            queue = nc.scalar if q < 2 else nc.sync
+            queue.dma_start(
+                out=out_2[0, 4 * q : 4 * q + 4, :].bitcast(I32), in_=out_plane[32 * q : 32 * q + 4, :].bitcast(I32)
+            )

@@ -143,7 +143,7 @@ def tile_moe_shf_glu_gelu_kernel(
             return words[:], scales[:]
 
         def deal(copy, out, in_):
-            copy(out=out.rearrange("p (t m) -> p t m", t=PACK), in_=in_.rearrange("p (m t) -> p t m", t=PACK))
+            copy(out=out.rearrange("p (t m) -> p m t", t=PACK), in_=in_.rearrange("p (m t) -> p m t", t=PACK))
 
         w2_dealt = [kept("w2_words%d" % e, [P, 2 * N], U8) for e in range(E)]
         w2_plane = [kept("w2_plane%d" % e, [P, N], U8) for e in range(E)]
@@ -170,22 +170,29 @@ def tile_moe_shf_glu_gelu_kernel(
             return (slots[i][0], slots[i][1], w1_of[i].bitcast(FP4X4), w13_plane[:, i * H : (i + 1) * H],
                     w3_of[i].bitcast(FP4X4), w13_plane[:, (E + i) * H : (E + i + 1) * H], h_codes[i][:], h_plane[i][:])
 
-        def first_layer(chunk, j):
-            tokens, token_scales, w1, w1_plane, w3, w3_plane = operands(chunk)[:6]
+        routed_act = {}
+
+        def routed_sums(acc, e, j, w, w_plane):
+            cols = slice(j * P, (j + 1) * P)
+            nc.tensor.matmul_mx(
+                out=acc[:], lhsT=slots[e][0][:, cols].bitcast(FP8X4), lhsT_scale=slots[e][1][:, cols],
+                rhs=w, rhs_scale=w_plane, start=True, stop=True,
+            )
+
+        def routed_gelu(e, j):
+            a1 = psum.tile([P, H], F32, name="a1", tag="a1", bufs=3)
+            routed_sums(a1, e, j, *operands(("e", e))[2:4])
+            routed_act[e, j] = act_tile([P, 2, P, 2])
+            nc.scalar.activation(routed_act[e, j][:], a1[:].rearrange("s (p u e) -> s u p e", u=2, e=2), GELU)
+
+        def routed_hidden(e, j):
+            chunk = ("e", e)
             if j == 0:
                 turned[chunk] = psum.tile([P, 2, 2, P], F32, name="turned", tag="turned", bufs=1)
-            cols = slice(j * P, (j + 1) * P)
-            a1 = psum.tile([P, H], F32, name="a1", tag="a1", bufs=3)
             a3 = psum.tile([P, H], F32, name="a3", tag="a3", bufs=2)
-            for acc, w, w_plane in ((a1, w1, w1_plane), (a3, w3, w3_plane)):
-                nc.tensor.matmul_mx(
-                    out=acc[:], lhsT=tokens[:, cols].bitcast(FP8X4), lhsT_scale=token_scales[:, cols],
-                    rhs=w, rhs_scale=w_plane, start=True, stop=True,
-                )
-            act = act_tile([P, 2, P, 2])
-            nc.scalar.activation(act[:], a1[:].rearrange("s (p u e) -> s u p e", u=2, e=2), GELU)
+            routed_sums(a3, e, j, *operands(chunk)[4:6])
             h = work.tile([P, 2, P, 2], BF16, name="h", tag="h")
-            nc.vector.tensor_tensor(h[:], a3[:].rearrange("s (p u e) -> s u p e", u=2, e=2), act[:], MULT)
+            nc.vector.tensor_tensor(h[:], a3[:].rearrange("s (p u e) -> s u p e", u=2, e=2), routed_act[e, j][:], MULT)
             for u in range(2):
                 nc.tensor.transpose(
                     turned[chunk][:, j, u, :], h[:, u].rearrange("s p e -> s (p e)").bitcast(F32), ident[:]
@@ -262,6 +269,12 @@ def tile_moe_shf_glu_gelu_kernel(
             gated[e, t] = kept("plain%d_%d" % (e, t), [P, C], F32)
             nc.scalar.copy(out=gated[e, t][:], in_=sums[e, t // 2][:, t % 2, :])
 
+        def plain_pair(e, pair):
+            both = kept("plain%d_pair%d" % (e, pair), [P, 2, C], F32)
+            nc.scalar.copy(out=both[:], in_=sums[e, pair][:])
+            for i in range(2):
+                gated[e, 2 * pair + i] = both[:, i, :]
+
         def scatter_weighed(e, t):
             lists = offsets[:, e * LIST_COLS : (e + 1) * LIST_COLS]
             nc.vector.tensor_tensor(window(t)[:].indirect(lists), gated[e, t][:], gate_tile[:, e * C : (e + 1) * C], MULT)
@@ -278,21 +291,27 @@ def tile_moe_shf_glu_gelu_kernel(
         slots[0] = gather(0)
         slots[1] = gather(1)
         slots[2] = gather(2)
-        first_layer(("e", 0), 0)
+        routed_gelu(0, 0)
+        routed_hidden(0, 0)
         deal_words(0, V)
-        first_layer(("e", 0), 1)
+        routed_gelu(0, 1)
+        routed_hidden(0, 1)
         deal_scales(0, V)
         quantise_hidden(("e", 0), S)
         second_layer(0, 1)
         second_layer(0, 0)
-        first_layer(("e", 1), 0)
-        first_layer(("e", 1), 1)
+        routed_gelu(1, 0)
+        routed_hidden(1, 0)
+        routed_gelu(1, 1)
+        routed_hidden(1, 1)
         deal_scales(2, V)
         deal(V, w1s[:], w1s_tile[:].bitcast(U32))
         weigh_pair(0, 1)
         quantise_hidden(("e", 1), S)
-        first_layer(("e", 2), 0)
-        first_layer(("e", 2), 1)
+        routed_gelu(2, 0)
+        routed_hidden(2, 0)
+        routed_gelu(2, 1)
+        routed_hidden(2, 1)
         shared_gelu(0, 0)
         shared_gelu(0, 1)
         shared_gelu(1, 0)
@@ -320,21 +339,21 @@ def tile_moe_shf_glu_gelu_kernel(
         deal(V, w2s[:], w2s_raw[:].bitcast(U32))
         shared_hidden(2, 0)
         shared_hidden(2, 1)
-        scatter(0, 0, "V")
-        weigh_pair(2, 1)
-        scatter(1, 0, "V")
-        weigh_pair(2, 0)
-        quantise_shared(2)
-        scatter(2, 0, "V")
+        scatter(0, 1, "S")
         scatter(0, 3, "S")
         scatter(0, 2, "S")
-        scatter(0, 1, "S")
+        scatter(0, 0, "V")
+        weigh_pair(2, 1)
+        scatter(1, 1, "V")
+        weigh_pair(2, 0)
+        scatter(1, 0, "V")
+        quantise_shared(2)
+        scatter(2, 1, "V")
+        scatter(2, 0, "V")
         scatter(1, 3, "S")
         scatter(1, 2, "S")
-        scatter(1, 1, "S")
         scatter(2, 3, "S")
         scatter(2, 2, "S")
-        scatter(2, 1, "S")
 
         def shared_product(out, t, cols):
             nc.tensor.matmul_mx(
@@ -347,7 +366,7 @@ def tile_moe_shf_glu_gelu_kernel(
         wide = [psum.tile([P, 2 * C], F32, name="ys_wide%d" % t, tag=("a1", "a3")[t % 2], bufs=(3, 2)[t % 2]) for t in range(PACK)]
         result = kept("result", [P, PACK, T], F32)
         out_rows = out_0.rearrange("(p t) n -> p t n", t=PACK)
-        order = (0, 3, 2, 1)
+        order = (0, 1, 3, 2)
         for t in order:
             shared_product(wide[t][:], t, slice(0, 2 * C))
             shared_product(narrow[t // 2][:, t % 2, :], t, slice(2 * C, T))
@@ -366,6 +385,12 @@ def tile_moe_shf_glu_gelu_kernel(
             nc.sync.dma_start(out=out_rows[:, t, :], in_=result[:, t, :])
         rounded = [kept("rounded%d" % c, [P, C, PACK], BF16) for c in range(E)]
 
+        def round_chunk(copy, c):
+            copy(
+                out=rounded[c][:].rearrange("p (g i) t -> p g t i", i=PACK),
+                in_=result[:, :, c * C : (c + 1) * C].rearrange("p t (g i) -> p g t i", i=PACK),
+            )
+
         def finish(c):
             cols = slice(c * C, (c + 1) * C)
             nc.vector.quantize_mx(
@@ -377,10 +402,10 @@ def tile_moe_shf_glu_gelu_kernel(
         for c in range(E):
             add(order[3], c)
             if c < 1:
-                S(out=rounded[c][:], in_=result[:, :, c * C : (c + 1) * C].rearrange("p t n -> p n t"))
+                round_chunk(S, c)
         nc.sync.dma_start(out=out_rows[:, order[3], :], in_=result[:, order[3], :])
         for c in (1, 2):
-            V(out=rounded[c][:], in_=result[:, :, c * C : (c + 1) * C].rearrange("p t n -> p n t"))
+            round_chunk(V, c)
         for c in range(E):
             finish(c)
         for q in range(4):

from contextlib import ExitStack

import concourse.mybir as mybir
from concourse.masks import make_identity

K, T, E, C, H, N = 512, 768, 3, 256, 512, 512
FLOPS = 2 * (T + E * C) * (2 * K * H + H * N)

F32 = mybir.dt.float32
BF16 = mybir.dt.bfloat16
I32 = mybir.dt.int32
U32 = mybir.dt.uint32
U16 = mybir.dt.uint16
U8 = mybir.dt.uint8
FP8X4 = mybir.dt.float8_e4m3fn_x4
FP4X4 = mybir.dt.float4_e2m1fn_x4
GELU = mybir.ActivationFunctionType.Gelu_apprx_tanh
COPY = mybir.ActivationFunctionType.Copy
MULT = mybir.AluOpType.mult
ADD = mybir.AluOpType.add

P = 128
PACK = 4
LIST_COLS = C // 16


def tile_moe_shf_glu_gelu_kernel(
    tc, x_words, x_scales, w1_words, w1_scales, w3_words, w3_scales, w2_words, w2_scales,
    w1s_words, w1s_scales, w3s_words, w3s_scales, w2s_words, w2s_scales, gate, offs,
    out_0, out_1, out_2,
):
    nc = tc.nc
    with ExitStack() as ctx:
        keep = ctx.enter_context(tc.tile_pool(name="keep", bufs=1))
        work = ctx.enter_context(tc.tile_pool(name="work", bufs=2))
        psum = ctx.enter_context(tc.psum_pool(name="psum", bufs=2))

        def kept(name, shape, dtype):
            return keep.tile(shape, dtype, name=name, align_bytes=64)

        def load_words(name, src, width):
            tile = kept(name, [P, width], U8)
            nc.sync.dma_start(out=tile[:].bitcast(I32), in_=src.bitcast(I32))
            return tile

        def load_scale_rows(plane, first, src, groups):
            for r in range(4):
                nc.sync.dma_start(
                    out=plane[first + r : P : 32, :].bitcast(I32).rearrange("q (g c) -> q g c", g=groups),
                    in_=src[:, r:16:4, :].bitcast(I32).rearrange("g q c -> q g c"),
                )

        offsets = keep.tile([P, T // 16], U16, name="offsets")
        x_plane = kept("x_plane", [P, T], U8)
        w13_plane = kept("w13_plane", [P, 2 * E * H], U8)
        w2_plane_raw = kept("w2_plane_raw", [P, (E - 1) * N], U8)
        packed_raw = kept("packed_raw", [P, N], U8)
        ident = kept("ident", [P, P], F32)
        for plane in (x_plane, w13_plane, w2_plane_raw, packed_raw):
            nc.vector.memset(plane[:].bitcast(I32), 0)

        make_identity(nc, ident[:])

        def stage_rows(queue, tile, sources, groups):
            for i, src in enumerate(sources):
                queue.dma_start(
                    out=tile[:, i * groups * H : (i + 1) * groups * H].bitcast(I32).rearrange("b (g c) -> b g c", g=groups),
                    in_=src.rearrange("g b c -> b g c").bitcast(I32),
                )

        def spread_rows(plane, tile):
            for r in range(4):
                nc.sync.dma_start(out=plane[r:P:32, :].bitcast(I32), in_=tile[r:16:4, :].bitcast(I32))

        def load_experts(name, src, first):
            count = E - first
            tile = kept(name, [P, count, 2 * H], U8)
            nc.sync.dma_start(
                out=tile[:].bitcast(I32), in_=src[first:E].rearrange("e s p c -> p (e s) c").bitcast(I32)
            )
            return tile

        by_group = "e s b c -> (e s) b c"
        staged = kept("staged", [16, 2 * E * H], U8)
        staged_packed = kept("staged_packed", [64, N], U8)

        def stage_packed(queue):
            for j, src in enumerate((w2_scales[E - 1, 0], w1s_scales[0], w3s_scales[0], w2s_scales[0])):
                queue.dma_start(
                    out=staged_packed[16 * j : 16 * j + 16, :].bitcast(I32),
                    in_=src.rearrange("(q r) c -> r q c", r=4).bitcast(I32),
                )

        def spread_packed():
            for q in range(4):
                nc.sync.dma_start(
                    out=packed_raw[32 * q : 32 * q + 16, :].bitcast(I32), in_=staged_packed[q:64:4, :].bitcast(I32)
                )

        x_tile = kept("x_tile", [P, T], I32)
        gate_tile = kept("gate_tile", [P, T], F32)
        stage_packed(nc.gpsimd)
        nc.sync.dma_start(offsets[:], offs)
        nc.sync.dma_start(out=x_tile[:], in_=x_words[0].rearrange("p t d -> p (t d)").bitcast(I32))
        stage_rows(nc.sync, staged, (w1_scales.rearrange(by_group), w3_scales.rearrange(by_group)), E)
        load_scale_rows(x_plane, 0, x_scales, 1)
        w1_first = load_words("w1_first", w1_words[0, 0], 2 * H)
        w3_first = load_words("w3_first", w3_words[0, 0], 2 * H)
        spread_rows(w13_plane, staged)
        w1_rest = load_experts("w1_rest", w1_words, 1)
        w3_rest = load_experts("w3_rest", w3_words, 1)
        w2_raw = load_experts("w2_raw", w2_words, 0)
        load_scale_rows(w2_plane_raw, 0, w2_scales[0 : E - 1].rearrange(by_group), E - 1)
        spread_packed()
        w1s_tile = load_words("w1s_tile", w1s_words[0].rearrange("p c d -> p (c d)"), PACK * H)
        nc.sync.dma_start(out=gate_tile[:], in_=gate)
        w3s_tile = load_words("w3s_tile", w3s_words[0].rearrange("p c d -> p (c d)"), PACK * H)
        w2s_raw = load_words("w2s_raw", w2s_words[0].rearrange("p c d -> p (c d)"), PACK * N)

        w1_of = [w1_first[:], w1_rest[:, 0, :], w1_rest[:, 1, :]]
        w3_of = [w3_first[:], w3_rest[:, 0, :], w3_rest[:, 1, :]]

        windows = {}
        holds = {}
        counter = [0]

        def act_tile(shape):
            n = counter[0]
            counter[0] = n + 1
            return keep.tile(shape, F32, name="act%d" % n, tag=holds.get(n, "act%d" % n), align_bytes=64)

        def window(t):
            if t not in windows:
                windows[t] = keep.tile([P, T], F32, name="window%d" % t, tag="window%d" % t, align_bytes=64)
            return windows[t]

        def gather(e):
            lists = offsets[:, e * LIST_COLS : (e + 1) * LIST_COLS]
            words = kept("slot_words%d" % e, [P, C], U32)
            scales = kept("slot_scales%d" % e, [P, C], U8)
            nc.vector.tensor_copy(words[:], x_tile[:].bitcast(U32).indirect(lists))
            nc.vector.tensor_copy(scales[:], x_plane[:].indirect(lists))
            return words[:], scales[:]

        def deal(copy, out, in_):
            copy(out=out.rearrange("p (t m) -> p m t", t=PACK), in_=in_.rearrange("p (m t) -> p m t", t=PACK))

        w2_dealt = [kept("w2_words%d" % e, [P, 2 * N], U8) for e in range(E)]
        w2_plane = [kept("w2_plane%d" % e, [P, N], U8) for e in range(E)]
        w2s = kept("w2s", [P, N], U32)
        w1s = kept("w1s", [P, H], U32)
        w3s = kept("w3s", [P, H], U32)
        packed = w2_plane[E - 1]

        def deal_words(e, copy):
            deal(copy, w2_dealt[e][:].bitcast(U16), w2_raw[:, e, :].bitcast(U16))

        def deal_scales(e, copy):
            deal(copy, w2_plane[e][:], w2_plane_raw[:, e * N : (e + 1) * N] if e < E - 1 else packed_raw[:])

        h_codes = [kept("h_codes%d" % e, [P, C], U32) for e in range(E)]
        h_plane = [kept("h_plane%d" % e, [P, C], U8) for e in range(E)]
        hs_codes = kept("hs_codes", [P, T], U32)
        hs_plane = kept("hs_plane", [P, T], U8)
        slots = {}
        turned = {}

        def operands(chunk):
            i = chunk[1]
            return (slots[i][0], slots[i][1], w1_of[i].bitcast(FP4X4), w13_plane[:, i * H : (i + 1) * H],
                    w3_of[i].bitcast(FP4X4), w13_plane[:, (E + i) * H : (E + i + 1) * H], h_codes[i][:], h_plane[i][:])

        routed_act = {}

        def routed_sums(acc, e, j, w, w_plane):
            cols = slice(j * P, (j + 1) * P)
            nc.tensor.matmul_mx(
                out=acc[:], lhsT=slots[e][0][:, cols].bitcast(FP8X4), lhsT_scale=slots[e][1][:, cols],
                rhs=w, rhs_scale=w_plane, start=True, stop=True,
            )

        def routed_gelu(e, j):
            a1 = psum.tile([P, H], F32, name="a1", tag="a1", bufs=3)
            routed_sums(a1, e, j, *operands(("e", e))[2:4])
            routed_act[e, j] = act_tile([P, 2, P, 2])
            nc.scalar.activation(routed_act[e, j][:], a1[:].rearrange("s (p u e) -> s u p e", u=2, e=2), GELU)

        def routed_hidden(e, j):
            chunk = ("e", e)
            if j == 0:
                turned[chunk] = psum.tile([P, 2, 2, P], F32, name="turned", tag="turned", bufs=1)
            a3 = psum.tile([P, H], F32, name="a3", tag="a3", bufs=2)
            routed_sums(a3, e, j, *operands(chunk)[4:6])
            h = work.tile([P, 2, P, 2], BF16, name="h", tag="h")
            nc.vector.tensor_tensor(h[:], a3[:].rearrange("s (p u e) -> s u p e", u=2, e=2), routed_act[e, j][:], MULT)
            for u in range(2):
                nc.tensor.transpose(
                    turned[chunk][:, j, u, :], h[:, u].rearrange("s p e -> s (p e)").bitcast(F32), ident[:]
                )

        def quantise_hidden(chunk, copy):
            codes, plane = operands(chunk)[6:]
            grouped = work.tile([P, C * PACK], BF16, name="grouped", tag="grouped", align_bytes=64)
            copy(
                out=grouped[:].bitcast(F32).rearrange("p (j s u) -> p j s u", j=2, u=2),
                in_=turned[chunk][:].rearrange("p j u s -> p j s u"),
            )
            nc.vector.quantize_mx(out=codes.bitcast(FP8X4), scales=plane, in_=grouped[:])

        shared_grouped = {}

        shared_act = {}

        def shared_sums(acc, w, first, c, j):
            cols = slice(c * C + j * P, c * C + (j + 1) * P)
            for t in range(PACK):
                nc.tensor.matmul_mx(
                    out=acc[:, t, :], lhsT=w[:, t * P : (t + 1) * P].bitcast(FP8X4),
                    lhsT_scale=packed[first:P, t * P : (t + 1) * P],
                    rhs=x_tile[:, cols].bitcast(FP8X4), rhs_scale=x_plane[:, cols], start=True, stop=True,
                )

        def shared_gelu(c, j):
            a1 = psum.tile([P, PACK, P], F32, name="a1", tag="a1", bufs=3)
            shared_sums(a1, w1s, 4, c, j)
            shared_act[c, j] = act_tile([P, P, PACK])
            nc.scalar.activation(shared_act[c, j][:], a1[:].rearrange("p t n -> p n t"), GELU)

        def shared_hidden(c, j):
            a3 = psum.tile([P, PACK, P], F32, name="a3", tag="a3", bufs=2)
            shared_sums(a3, w3s, 8, c, j)
            if j == 0:
                shared_grouped[c] = work.tile([P, 2, P, PACK], BF16, name="grouped", tag="grouped", align_bytes=64)
            nc.vector.tensor_tensor(shared_grouped[c][:, j], a3[:].rearrange("p t n -> p n t"), shared_act[c, j][:], MULT)

        def quantise_shared(c):
            cols = slice(c * C, (c + 1) * C)
            nc.vector.quantize_mx(
                out=hs_codes[:, cols].bitcast(FP8X4), scales=hs_plane[:, cols],
                in_=shared_grouped[c][:].rearrange("p j n t -> p (j n t)"),
            )

        gated = {}
        sums = {}

        def second_layer(e, pair):
            y = psum.tile([P, 2, C], F32, name="y", tag="y", bufs=2)
            for i in range(2):
                t = 2 * pair + i
                nc.tensor.matmul_mx(
                    out=y[:, i, :], lhsT=w2_dealt[e][:, t * 2 * P : (t + 1) * 2 * P].bitcast(FP4X4),
                    lhsT_scale=w2_plane[e][:, t * P : (t + 1) * P],
                    rhs=h_codes[e][:].bitcast(FP8X4), rhs_scale=h_plane[e][:], start=True, stop=True,
                )
            sums[e, pair] = y

        def weigh(e, t):
            gated[e, t] = kept("gated%d_%d" % (e, t), [P, C], F32)
            nc.vector.tensor_tensor(gated[e, t][:], sums[e, t // 2][:, t % 2, :], gate_tile[:, e * C : (e + 1) * C], MULT)

        def weigh_pair(e, pair):
            both = keep.tile([P, 2, C], F32, name="gated%d_pair%d" % (e, pair), tag="gated%d%d" % (e, pair), align_bytes=64)
            gates = gate_tile[:, e * C : (e + 1) * C].unsqueeze(1).to_broadcast([P, 2, C])
            nc.vector.tensor_tensor(both[:], sums[e, pair][:], gates, MULT)
            for i in range(2):
                gated[e, 2 * pair + i] = both[:, i, :]

        def plain(e, t):
            gated[e, t] = kept("plain%d_%d" % (e, t), [P, C], F32)
            nc.scalar.copy(out=gated[e, t][:], in_=sums[e, t // 2][:, t % 2, :])

        def plain_pair(e, pair):
            both = kept("plain%d_pair%d" % (e, pair), [P, 2, C], F32)
            nc.scalar.copy(out=both[:], in_=sums[e, pair][:])
            for i in range(2):
                gated[e, 2 * pair + i] = both[:, i, :]

        def scatter_weighed(e, t):
            lists = offsets[:, e * LIST_COLS : (e + 1) * LIST_COLS]
            nc.vector.tensor_tensor(window(t)[:].indirect(lists), gated[e, t][:], gate_tile[:, e * C : (e + 1) * C], MULT)

        def scatter(e, t, engine):
            lists = offsets[:, e * LIST_COLS : (e + 1) * LIST_COLS]
            values = gated[e, t][:]
            if engine == "V":
                nc.vector.tensor_copy(window(t)[:].indirect(lists), values)
            else:
                nc.scalar.activation(window(t)[:].indirect(lists), values, COPY)

        V, S, G = nc.vector.tensor_copy, nc.scalar.copy, nc.gpsimd.tensor_copy
        slots[0] = gather(0)
        slots[1] = gather(1)
        slots[2] = gather(2)
        routed_gelu(0, 0)
        routed_hidden(0, 0)
        deal_words(0, V)
        routed_gelu(0, 1)
        routed_hidden(0, 1)
        deal_scales(0, V)
        quantise_hidden(("e", 0), S)
        second_layer(0, 1)
        second_layer(0, 0)
        routed_gelu(1, 0)
        routed_hidden(1, 0)
        routed_gelu(1, 1)
        routed_hidden(1, 1)
        deal_scales(2, V)
        deal(V, w1s[:], w1s_tile[:].bitcast(U32))
        weigh_pair(0, 1)
        quantise_hidden(("e", 1), S)
        routed_gelu(2, 0)
        routed_hidden(2, 0)
        routed_gelu(2, 1)
        routed_hidden(2, 1)
        shared_gelu(0, 0)
        shared_gelu(0, 1)
        shared_gelu(1, 0)
        shared_gelu(1, 1)
        shared_gelu(2, 0)
        shared_gelu(2, 1)
        quantise_hidden(("e", 2), S)
        weigh_pair(0, 0)
        deal_words(1, V)
        deal_scales(1, V)
        second_layer(1, 1)
        second_layer(1, 0)
        deal(V, w3s[:], w3s_tile[:].bitcast(U32))
        shared_hidden(0, 0)
        shared_hidden(0, 1)
        weigh_pair(1, 1)
        quantise_shared(0)
        shared_hidden(1, 0)
        shared_hidden(1, 1)
        weigh_pair(1, 0)
        deal_words(2, V)
        second_layer(2, 1)
        second_layer(2, 0)
        quantise_shared(1)
        deal(V, w2s[:], w2s_raw[:].bitcast(U32))
        shared_hidden(2, 0)
        shared_hidden(2, 1)
        scatter(0, 1, "S")
        scatter(0, 3, "S")
        scatter(0, 2, "S")
        scatter(0, 0, "V")
        weigh_pair(2, 1)
        scatter(1, 1, "V")
        weigh_pair(2, 0)
        scatter(1, 0, "V")
        quantise_shared(2)
        scatter(2, 1, "V")
        scatter(2, 0, "V")
        scatter(1, 3, "S")
        scatter(1, 2, "S")
        scatter(2, 3, "S")
        scatter(2, 2, "S")

        def shared_product(out, t, cols):
            nc.tensor.matmul_mx(
                out=out, lhsT=w2s[:, t * P : (t + 1) * P].bitcast(FP8X4),
                lhsT_scale=packed[12:P, t * P : (t + 1) * P],
                rhs=hs_codes[:, cols].bitcast(FP8X4), rhs_scale=hs_plane[:, cols], start=True, stop=True,
            )

        narrow = [psum.tile([P, 2, C], F32, name="ys_narrow%d" % i, tag="y", bufs=2) for i in range(2)]
        wide = [psum.tile([P, 2 * C], F32, name="ys_wide%d" % t, tag=("a1", "a3")[t % 2], bufs=(3, 2)[t % 2]) for t in range(PACK)]
        result = kept("result", [P, PACK, T], F32)
        out_rows = out_0.rearrange("(p t) n -> p t n", t=PACK)
        order = (0, 1, 3, 2)
        for t in order:
            shared_product(wide[t][:], t, slice(0, 2 * C))
            shared_product(narrow[t // 2][:, t % 2, :], t, slice(2 * C, T))
        out_codes = kept("out_codes", [P, T], U32)
        out_plane = kept("out_plane", [P, T], U8)
        out_words = out_1[0].rearrange("p t d -> p (t d)").bitcast(I32)

        def add(t, c):
            cols = slice(c * C, (c + 1) * C)
            ys = narrow[t // 2][:, t % 2, :] if c == 2 else wide[t][:, cols]
            nc.vector.tensor_tensor(result[:, t, cols], ys, windows[t][:, cols], ADD)

        for t in order[:3]:
            nc.vector.tensor_tensor(result[:, t, 0 : 2 * C], wide[t][:], windows[t][:, 0 : 2 * C], ADD)
            add(t, 2)
            nc.sync.dma_start(out=out_rows[:, t, :], in_=result[:, t, :])
        rounded = [kept("rounded%d" % c, [P, C, PACK], BF16) for c in range(E)]

        def round_chunk(copy, c):
            copy(
                out=rounded[c][:].rearrange("p (g i) t -> p g t i", i=PACK),
                in_=result[:, :, c * C : (c + 1) * C].rearrange("p t (g i) -> p g t i", i=PACK),
            )

        def finish(c):
            cols = slice(c * C, (c + 1) * C)
            nc.vector.quantize_mx(
                out=out_codes[:, cols].bitcast(FP8X4), scales=out_plane[:, cols],
                in_=rounded[c][:].rearrange("p n t -> p (n t)"),
            )
            nc.sync.dma_start(out=out_words[:, cols], in_=out_codes[:, cols].bitcast(I32))

        for c in range(E):
            add(order[3], c)
            if c < 1:
                round_chunk(S, c)
        nc.sync.dma_start(out=out_rows[:, order[3], :], in_=result[:, order[3], :])
        for c in (1, 2):
            round_chunk(V, c)
        for c in range(E):
            finish(c)
        for q in range(4):
            queue = nc.scalar if q < 2 else nc.sync
            queue.dma_start(
                out=out_2[0, 4 * q : 4 * q + 4, :].bitcast(I32), in_=out_plane[32 * q : 32 * q + 4, :].bitcast(I32)
            )
